import numpy as np
import ml_dtypes


def mxq(x, axis, fmt="e4m3"):
    dtype, down = {"e4m3": (ml_dtypes.float8_e4m3fn, 7), "e5m2": (ml_dtypes.float8_e5m2, 14)}[fmt]
    v = np.moveaxis(np.asarray(x, np.float32).astype(ml_dtypes.bfloat16).astype(np.float64), axis, -1)
    blocks = v.reshape(v.shape[:-1] + (-1, 32))
    amax = np.abs(blocks).max(-1, keepdims=True)
    byte = np.maximum(np.where(amax > 0, np.frexp(amax)[1] - 1 + 127, 0) - down, 1)
    scale = np.exp2(byte - 127.0)
    codes = (blocks / scale).astype(np.float32).astype(dtype).astype(np.float64)
    return np.moveaxis((codes * scale).reshape(v.shape), -1, axis)


WIDE = False


def mx_kscale(k):
    if not WIDE:
        return np.ones(k)
    levels = np.array([10, -10, 5, -5, 0])
    if k % 512:
        return np.exp2(np.random.permutation(np.resize(levels, k // 32))).repeat(32)
    a = np.empty((k // 512, 16))
    for p in range(k // 512):
        a[p, :8] = np.random.permutation(np.resize(levels, 8))
        for g in range(8):
            far = levels[np.abs(levels - a[p, g]) >= 10]
            a[p, g + 8] = far[np.random.randint(len(far))]
    return np.exp2(a.ravel()).repeat(32)


def f64(x):
    return np.asarray(x).astype(np.float64)


def striped(idx):
    return np.tile(np.asarray(idx).reshape(-1, 16).T, (8, 1)).astype(np.uint16)


def unstriped(offs):
    return offs[:16].T.reshape(-1).astype(np.int64)


E2M1 = np.array([0.0, 0.5, 1.0, 1.5, 2.0, 3.0, 4.0, 6.0, -0.0, -0.5, -1.0, -1.5, -2.0, -3.0, -4.0, -6.0])


def pack_weight(w, fmt):
    k, n = w.shape
    w = f64(np.asarray(w, np.float32).astype(ml_dtypes.bfloat16)).reshape(k // 32, 32, n)
    amax = np.abs(w).max(1)
    if fmt == "e4m3":
        byte = np.frexp(amax)[1] - 1 + 127 - 7
    else:
        mant, ex = np.frexp(amax / 6.0)
        byte = np.where(mant > 0.5, ex, ex - 1) + 127
    byte = np.clip(np.where(amax > 0, byte, 1), 1, 254)
    scaled = (w * np.exp2(127.0 - byte)[:, None, :]).reshape(k, n).astype(np.float32)
    by_word = np.ascontiguousarray(scaled.reshape(k // 512, 128, 4, n).transpose(0, 1, 3, 2))
    if fmt == "e4m3":
        words = by_word.astype(ml_dtypes.float8_e4m3fn).view(np.uint8)
    else:
        c = by_word.astype(ml_dtypes.float4_e2m1fn).view(np.uint8) & 0xF
        words = (c[..., 0::2] | (c[..., 1::2] << 4)).reshape(k // 512, 128, 2 * n)
    return np.ascontiguousarray(words), np.ascontiguousarray(byte.astype(np.uint8).reshape(k // 512, 16, n))


def unpack_weight(words, scales, fmt):
    g, _, n = scales.shape
    words = np.ascontiguousarray(words).reshape(g, 128, n, -1)
    if fmt == "e4m3":
        vals = words.view(ml_dtypes.float8_e4m3fn).astype(np.float64)
    else:
        nib = np.empty((g, 128, n, 4), np.uint8)
        nib[..., 0::2] = words & 0xF
        nib[..., 1::2] = words >> 4
        vals = E2M1[nib]
    vals = vals * np.repeat(np.exp2(scales.astype(np.float64) - 127.0), 8, axis=1)[..., None]
    return vals.transpose(0, 1, 3, 2).reshape(g * 512, n)


D, V, I, Q, T = 512, 2048, 512, 128, 4096


def setup_inputs():
    n = np.random.standard_normal
    idx = np.random.permutation(T)[:V]
    idx2 = np.random.randint(0, V, I)
    fd = mx_kscale(D)
    vocp = pack_weight(n((D, T)) / fd[:, None], "e2m1")
    return {
        "hid": (n((D, Q)) * 1.0 / np.sqrt(D) * fd[:, None]).astype(np.float32),
        "voc_words": vocp[0],
        "voc_scales": vocp[1],
        "old": (np.random.uniform(0.0, 1.0, (Q, I))).astype(np.float32),
        "skip": (np.random.uniform(0.0, 1.0, (1, I))).astype(np.float32),
        "offs": striped(idx),
        "offs2": striped(idx2),
    }


def reference(hid, voc_words, voc_scales, old, skip, offs, offs2):
    idx = unstriped(offs)
    idx2 = unstriped(offs2)
    vocu = unpack_weight(voc_words, voc_scales, "e2m1")
    hidq = mxq(f64(hid), 0, "e4m3")
    vocidxg = vocu[:, idx]
    a = hidq.T @ vocidxg
    p = np.exp(a - np.max(a, axis=1, keepdims=True))
    w = p / np.sum(p, axis=1, keepdims=True) * 2048.0
    b1 = np.pad(f64(old), ((0, 0), (1, 0)))[:, :I]
    b2 = np.pad(f64(old), ((0, 0), (2, 0)))[:, :I]
    y = (f64(old) + b1 + b2 * f64(skip)) * w[:, idx2]
    return y

@@ -1,0 +1,177 @@
+from contextlib import ExitStack
+
+import concourse.mybir as mybir
+from concourse.masks import make_identity
+
+D, V, L, Q, T = 512, 2048, 512, 128, 4096
+
+F32 = mybir.dt.float32
+BF16 = mybir.dt.bfloat16
+I32 = mybir.dt.int32
+U32 = mybir.dt.uint32
+U16 = mybir.dt.uint16
+U8 = mybir.dt.uint8
+FP8X4 = mybir.dt.float8_e4m3fn_x4
+FP4X4 = mybir.dt.float4_e2m1fn_x4
+ALU = mybir.AluOpType
+ACT = mybir.ActivationFunctionType
+AXIS_X = mybir.AxisListType.X
+
+P = 128
+PACK = 4
+N = 512
+CHUNKS = V // N
+LIST_COL = 16
+PAD = 8
+WORD_GATHER = 1024
+OUT_PIECES = 2
+
+FLOPS = 2 * D * Q * V
+
+
+def tile_attend_labelforward_kernel(tc, hid, voc_words, voc_scales, old, skip, offs, offs2, out):
+    nc = tc.nc
+    with ExitStack() as ctx:
+        lists = ctx.enter_context(tc.tile_pool(name="lists", bufs=1))
+        sb = ctx.enter_context(tc.tile_pool(name="sb", bufs=1))
+        ps = ctx.enter_context(tc.psum_pool(name="ps", bufs=1))
+
+        entry_list = lists.tile([P, V // LIST_COL], U16, name="entry_list")
+        label_list = lists.tile([P, L // LIST_COL], U16, name="label_list")
+
+        scale_store = sb.tile([P, T], U8, name="scale_store", align_bytes=64)
+        old_pad = sb.tile([P, PAD + L], F32, name="old_pad")
+        skip_rows = sb.tile([P, P], F32, name="skip_rows")
+        ident = sb.tile([P, P], F32, name="ident")
+        voc_plane = sb.tile([P, V], U8, name="voc_plane", align_bytes=64)
+
+        nc.vector.memset(scale_store[:].bitcast(I32), 0)
+        nc.sync.dma_start(entry_list[:], offs)
+        nc.sync.dma_start(scale_store[0:P:8, :].bitcast(I32), voc_scales[0].bitcast(I32))
+        nc.sync.dma_start(label_list[:], offs2)
+
+        nc.vector.memset(old_pad[:, 0 : 2 * PAD], 0.0)
+        warm_out = sb.tile([P, 1], F32, name="warm_out", tag="hid_raw")
+        warm_sum = sb.tile([P, 1], F32, name="warm_sum", tag="word_store", align_bytes=64)
+        nc.scalar.activation(warm_out[:], old_pad[:, PAD : PAD + 1], ACT.Exp, accum_out=warm_sum[:])
+        hid_raw = sb.tile([P, PACK, Q], F32, name="hid_raw", tag="hid_raw")
+        word_store = sb.tile([P, T], U16, name="word_store", tag="word_store", align_bytes=64)
+        nc.scalar.dma_start(hid_raw[:], hid.rearrange("(p t) q -> p t q", t=PACK))
+        nc.scalar.dma_start(word_store[:].bitcast(I32), voc_words[0].bitcast(I32))
+        nc.scalar.dma_start(old_pad[:, PAD:], old)
+
+        nc.vector.memset(voc_plane[:].bitcast(I32), 0)
+        nc.vector.memset(skip_rows[:], 0.0)
+        nc.vector.memset(ident[:], 0.0)
+        make_identity(nc, ident[:], nomemset=True)
+        nc.sync.dma_start(skip_rows[0 : L // P, :], skip.rearrange("o (j p) -> (o j) p", p=P))
+
+
+        scale_picked = sb.tile([P, V], U8, name="scale_picked", align_bytes=64)
+        nc.vector.tensor_copy(scale_picked[:], scale_store[:].indirect(entry_list[:]))
+        for j in range(4):
+            nc.sync.dma_start(voc_plane[j:P:32, :].bitcast(I32), scale_picked[8 * j : P : 32, :].bitcast(I32))
+
+        hid_grouped = sb.tile([P, Q, PACK], BF16, name="hid_grouped", align_bytes=64)
+        nc.scalar.copy(hid_grouped[:], hid_raw[:].rearrange("p t q -> p q t"))
+        hid_codes = sb.tile([P, Q], U32, name="hid_codes", align_bytes=64)
+        hid_plane = sb.tile([P, Q], U8, name="hid_plane", align_bytes=64)
+        nc.vector.quantize_mx(
+            out=hid_codes[:].bitcast(FP8X4),
+            scales=hid_plane[:],
+            in_=hid_grouped[:].rearrange("p q t -> p (q t)"),
+        )
+
+        picked = []
+        for g in range(V // WORD_GATHER):
+            words = sb.tile([P, WORD_GATHER], U16, name=f"words{g}", align_bytes=64)
+            cols = slice(g * WORD_GATHER // LIST_COL, (g + 1) * WORD_GATHER // LIST_COL)
+            nc.vector.tensor_copy(words[:], word_store[:].indirect(entry_list[:, cols]))
+            picked.append(words)
+
+        skip_ps = ps.tile([P, P], F32, name="skip_ps")
+        nc.tensor.transpose(skip_ps[:], skip_rows[:], ident[:])
+        skip_cols = sb.tile([P, L // P], F32, name="skip_cols")
+        nc.scalar.copy(skip_cols[:], skip_ps[:, 0 : L // P])
+
+        far_ps = ps.tile([P, L], F32, name="far_ps")
+        near_ps = ps.tile([P, L], F32, name="near_ps")
+        for j in range(L // P):
+            lo = PAD + j * P
+            nc.tensor.transpose(far_ps[:, j * P : (j + 1) * P], old_pad[:, lo - 2 : lo - 2 + P], ident[:])
+        for j in range(L // P):
+            lo = PAD + j * P
+            for back in range(2):
+                nc.tensor.matmul(
+                    near_ps[:, j * P : (j + 1) * P],
+                    old_pad[:, lo - back : lo - back + P],
+                    ident[:],
+                    start=(back == 0),
+                    stop=(back == 1),
+                    is_transpose=True,
+                )
+        far_t = sb.tile([P, L], F32, name="far_t")
+        near_t = sb.tile([P, L], F32, name="near_t")
+        for j in range(L // P):
+            blk = slice(j * P, (j + 1) * P)
+            nc.scalar.activation(far_t[:, blk], far_ps[:, blk], ACT.Copy, scale=skip_cols[:, j : j + 1])
+        nc.scalar.copy(near_t[:], near_ps[:])
+        reach_ps = ps.tile([P, L], F32, name="reach_ps")
+        for j in range(L // P):
+            blk = slice(j * P, (j + 1) * P)
+            nc.tensor.matmul(reach_ps[:, blk], near_t[:, blk], ident[:], start=True, stop=False, is_transpose=True)
+            nc.tensor.matmul(reach_ps[:, blk], far_t[:, blk], ident[:], start=False, stop=True, is_transpose=True)
+        reach = sb.tile([P, L], F32, name="reach")
+        nc.scalar.copy(reach[:], reach_ps[:])
+
+        neg_max = sb.tile([P, CHUNKS], F32, name="neg_max")
+        sums = sb.tile([P, CHUNKS], F32, name="sums")
+        exps = []
+        for c in range(CHUNKS):
+            g, lo = divmod(c * N, WORD_GATHER)
+            score = ps.tile([P, N], F32, name=f"score{c}")
+            nc.tensor.matmul_mx(
+                out=score[:],
+                lhsT=hid_codes[:].bitcast(FP8X4),
+                lhsT_scale=hid_plane[:],
+                rhs=picked[g][:, lo : lo + N].bitcast(FP4X4),
+                rhs_scale=voc_plane[:, c * N : (c + 1) * N],
+                start=True,
+                stop=True,
+            )
+            nc.vector.tensor_reduce(neg_max[:, c : c + 1], score[:], AXIS_X, ALU.max, negate=True)
+            e = sb.tile([P, N], F32, name=f"exp{c}")
+            nc.scalar.activation(e[:], score[:], ACT.Exp, bias=neg_max[:, c : c + 1], accum_out=sums[:, c : c + 1])
+            exps.append(e)
+
+        neg_top = sb.tile([P, 1], F32, name="neg_top")
+        nc.vector.tensor_reduce(neg_top[:], neg_max[:], AXIS_X, ALU.min)
+        lift = sb.tile([P, CHUNKS], F32, name="lift")
+        nc.scalar.activation(lift[:], neg_max[:], ACT.Exp, bias=neg_top[:], scale=-1.0)
+        shares = sb.tile([P, CHUNKS], F32, name="shares")
+        total = sb.tile([P, 1], F32, name="total")
+        nc.vector.scalar_tensor_tensor(
+            shares[:], sums[:], 1.0 / V, lift[:], ALU.mult, ALU.mult, accum_out=total[:]
+        )
+        inv = sb.tile([P, 1], F32, name="inv")
+        nc.vector.reciprocal(inv[:], total[:])
+
+        w = sb.tile([P, V], F32, name="w")
+        last = CHUNKS - 1
+        last_factor = sb.tile([P, 1], F32, name="last_factor")
+        nc.scalar.activation(last_factor[:], lift[:, last : last + 1], ACT.Copy, scale=inv[:])
+        nc.scalar.activation(w[:, last * N :], exps[last][:], ACT.Copy, scale=last_factor[:])
+        for c in range(last):
+            nc.vector.tensor_scalar(
+                w[:, c * N : (c + 1) * N], exps[c][:], lift[:, c : c + 1], inv[:], ALU.mult, ALU.mult
+            )
+
+        piece = L // OUT_PIECES
+        for h in range(OUT_PIECES):
+            res = sb.tile([P, piece], F32, name=f"res{h}")
+            cols = slice(h * piece // LIST_COL, (h + 1) * piece // LIST_COL)
+            nc.vector.tensor_tensor(
+                res[:], w[:].indirect(label_list[:, cols]), reach[:, h * piece : (h + 1) * piece], ALU.mult
+            )
+            queue = nc.sync if h == OUT_PIECES - 1 else nc.scalar
+            queue.dma_start(out[:, h * piece : (h + 1) * piece], res[:])

@@ -19,14 +19,18 @@ AXIS_X = mybir.AxisListType.X
 
 P = 128
 PACK = 4
-N = 512
-CHUNKS = V // N
 LIST_COL = 16
 PAD = 8
-WORD_GATHER = 1024
-OUT_PIECES = 2
+ROW0 = P - 16
+SCALE_GATHERS = 2
+SPANS = ((0, 512), (512, 1024), (1024, 1536), (1536, 1792), (1792, 2048))
+OUT_PIECES = ((0, 384), (384, 512))
 
 FLOPS = 2 * D * Q * V
+
+
+def listed(lo, hi):
+    return slice(lo // LIST_COL, hi // LIST_COL)
 
 
 def tile_attend_labelforward_kernel(tc, hid, voc_words, voc_scales, old, skip, offs, offs2, out):
@@ -44,21 +48,18 @@ def tile_attend_labelforward_kernel(tc, hid, voc_words, voc_scales, old, skip, o
         skip_rows = sb.tile([P, P], F32, name="skip_rows")
         ident = sb.tile([P, P], F32, name="ident")
         voc_plane = sb.tile([P, V], U8, name="voc_plane", align_bytes=64)
+        hid_raw = sb.tile([P, PACK, Q], F32, name="hid_raw", tag="stage1", align_bytes=64)
 
-        nc.vector.memset(scale_store[:].bitcast(I32), 0)
+        word_store = sb.tile([P, T], U16, name="word_store", align_bytes=64)
         nc.sync.dma_start(entry_list[:], offs)
-        nc.sync.dma_start(scale_store[0:P:8, :].bitcast(I32), voc_scales[0].bitcast(I32))
+        nc.scalar.dma_start(scale_store[ROW0:, :].bitcast(I32), voc_scales[0].bitcast(I32))
+        nc.scalar.dma_start(hid_raw[:], hid.rearrange("(p t) q -> p t q", t=PACK))
+        nc.scalar.dma_start(old_pad[:, PAD:], old)
+        nc.scalar.dma_start(word_store[:].bitcast(I32), voc_words[0].bitcast(I32))
         nc.sync.dma_start(label_list[:], offs2)
 
-        nc.vector.memset(old_pad[:, 0 : 2 * PAD], 0.0)
-        warm_out = sb.tile([P, 1], F32, name="warm_out", tag="hid_raw")
-        warm_sum = sb.tile([P, 1], F32, name="warm_sum", tag="word_store", align_bytes=64)
-        nc.scalar.activation(warm_out[:], old_pad[:, PAD : PAD + 1], ACT.Exp, accum_out=warm_sum[:])
-        hid_raw = sb.tile([P, PACK, Q], F32, name="hid_raw", tag="hid_raw")
-        word_store = sb.tile([P, T], U16, name="word_store", tag="word_store", align_bytes=64)
-        nc.scalar.dma_start(hid_raw[:], hid.rearrange("(p t) q -> p t q", t=PACK))
-        nc.scalar.dma_start(word_store[:].bitcast(I32), voc_words[0].bitcast(I32))
-        nc.scalar.dma_start(old_pad[:, PAD:], old)
+        nc.vector.memset(scale_store[0:ROW0, :].bitcast(I32), 0)
+        nc.vector.memset(old_pad[:, 0:PAD], 0.0)
 
         nc.vector.memset(voc_plane[:].bitcast(I32), 0)
         nc.vector.memset(skip_rows[:], 0.0)
@@ -66,14 +67,20 @@ def tile_attend_labelforward_kernel(tc, hid, voc_words, voc_scales, old, skip, o
         make_identity(nc, ident[:], nomemset=True)
         nc.sync.dma_start(skip_rows[0 : L // P, :], skip.rearrange("o (j p) -> (o j) p", p=P))
 
-
-        scale_picked = sb.tile([P, V], U8, name="scale_picked", align_bytes=64)
-        nc.vector.tensor_copy(scale_picked[:], scale_store[:].indirect(entry_list[:]))
-        for j in range(4):
-            nc.sync.dma_start(voc_plane[j:P:32, :].bitcast(I32), scale_picked[8 * j : P : 32, :].bitcast(I32))
-
-        hid_grouped = sb.tile([P, Q, PACK], BF16, name="hid_grouped", align_bytes=64)
+        hid_grouped = sb.tile([P, Q, PACK], BF16, name="hid_grouped", tag="words_a", align_bytes=64)
         nc.scalar.copy(hid_grouped[:], hid_raw[:].rearrange("p t q -> p q t"))
+
+        def gather_scales(g):
+            width = V // SCALE_GATHERS
+            lo, hi = g * width, (g + 1) * width
+            picked_scales = sb.tile([P, width], U8, name=f"picked_scales{g}", tag=f"stage{g}", align_bytes=64)
+            nc.vector.tensor_copy(picked_scales[:], scale_store[:].indirect(entry_list[:, listed(lo, hi)]))
+            for j in range(4):
+                nc.sync.dma_start(
+                    voc_plane[j:P:32, lo:hi].bitcast(I32), picked_scales[ROW0 + j : P : 4, :].bitcast(I32)
+                )
+
+        gather_scales(0)
         hid_codes = sb.tile([P, Q], U32, name="hid_codes", align_bytes=64)
         hid_plane = sb.tile([P, Q], U8, name="hid_plane", align_bytes=64)
         nc.vector.quantize_mx(
@@ -81,15 +88,10 @@ def tile_attend_labelforward_kernel(tc, hid, voc_words, voc_scales, old, skip, o
             scales=hid_plane[:],
             in_=hid_grouped[:].rearrange("p q t -> p (q t)"),
         )
+        gather_scales(1)
 
-        picked = []
-        for g in range(V // WORD_GATHER):
-            words = sb.tile([P, WORD_GATHER], U16, name=f"words{g}", align_bytes=64)
-            cols = slice(g * WORD_GATHER // LIST_COL, (g + 1) * WORD_GATHER // LIST_COL)
-            nc.vector.tensor_copy(words[:], word_store[:].indirect(entry_list[:, cols]))
-            picked.append(words)
 
-        skip_ps = ps.tile([P, P], F32, name="skip_ps")
+        skip_ps = ps.tile([P, P], F32, name="skip_ps", tag="reach_ps")
         nc.tensor.transpose(skip_ps[:], skip_rows[:], ident[:])
         skip_cols = sb.tile([P, L // P], F32, name="skip_cols")
         nc.scalar.copy(skip_cols[:], skip_ps[:, 0 : L // P])
@@ -116,7 +118,7 @@ def tile_attend_labelforward_kernel(tc, hid, voc_words, voc_scales, old, skip, o
             blk = slice(j * P, (j + 1) * P)
             nc.scalar.activation(far_t[:, blk], far_ps[:, blk], ACT.Copy, scale=skip_cols[:, j : j + 1])
         nc.scalar.copy(near_t[:], near_ps[:])
-        reach_ps = ps.tile([P, L], F32, name="reach_ps")
+        reach_ps = ps.tile([P, L], F32, name="reach_ps", tag="reach_ps")
         for j in range(L // P):
             blk = slice(j * P, (j + 1) * P)
             nc.tensor.matmul(reach_ps[:, blk], near_t[:, blk], ident[:], start=True, stop=False, is_transpose=True)
@@ -124,31 +126,47 @@ def tile_attend_labelforward_kernel(tc, hid, voc_words, voc_scales, old, skip, o
         reach = sb.tile([P, L], F32, name="reach")
         nc.scalar.copy(reach[:], reach_ps[:])
 
-        neg_max = sb.tile([P, CHUNKS], F32, name="neg_max")
-        sums = sb.tile([P, CHUNKS], F32, name="sums")
+        neg_max = sb.tile([P, len(SPANS)], F32, name="neg_max")
+        sums = sb.tile([P, len(SPANS)], F32, name="sums")
         exps = []
-        for c in range(CHUNKS):
-            g, lo = divmod(c * N, WORD_GATHER)
-            score = ps.tile([P, N], F32, name=f"score{c}")
+
+        def gather_words(lo, hi, tag):
+            words = sb.tile([P, hi - lo], U16, name=f"words{lo}", tag=tag, align_bytes=64)
+            nc.vector.tensor_copy(words[:], word_store[:].indirect(entry_list[:, listed(lo, hi)]))
+            return words, lo
+
+        def score_span(c, gathered):
+            words, base = gathered
+            lo, hi = SPANS[c]
+            score = ps.tile([P, hi - lo], F32, name=f"score{c}")
             nc.tensor.matmul_mx(
                 out=score[:],
                 lhsT=hid_codes[:].bitcast(FP8X4),
                 lhsT_scale=hid_plane[:],
-                rhs=picked[g][:, lo : lo + N].bitcast(FP4X4),
-                rhs_scale=voc_plane[:, c * N : (c + 1) * N],
+                rhs=words[:, lo - base : hi - base].bitcast(FP4X4),
+                rhs_scale=voc_plane[:, lo:hi],
                 start=True,
                 stop=True,
             )
             nc.vector.tensor_reduce(neg_max[:, c : c + 1], score[:], AXIS_X, ALU.max, negate=True)
-            e = sb.tile([P, N], F32, name=f"exp{c}")
+            e = sb.tile([P, hi - lo], F32, name=f"exp{c}")
             nc.scalar.activation(e[:], score[:], ACT.Exp, bias=neg_max[:, c : c + 1], accum_out=sums[:, c : c + 1])
             exps.append(e)
 
+        first = gather_words(0, 1024, "words_a")
+        second = gather_words(1024, 1536, "stage0")
+        score_span(0, first)
+        score_span(1, first)
+        third = gather_words(1536, 2048, "words_a")
+        score_span(2, second)
+        score_span(3, third)
+        score_span(4, third)
+
         neg_top = sb.tile([P, 1], F32, name="neg_top")
         nc.vector.tensor_reduce(neg_top[:], neg_max[:], AXIS_X, ALU.min)
-        lift = sb.tile([P, CHUNKS], F32, name="lift")
+        lift = sb.tile([P, len(SPANS)], F32, name="lift")
         nc.scalar.activation(lift[:], neg_max[:], ACT.Exp, bias=neg_top[:], scale=-1.0)
-        shares = sb.tile([P, CHUNKS], F32, name="shares")
+        shares = sb.tile([P, len(SPANS)], F32, name="shares")
         total = sb.tile([P, 1], F32, name="total")
         nc.vector.scalar_tensor_tensor(
             shares[:], sums[:], 1.0 / V, lift[:], ALU.mult, ALU.mult, accum_out=total[:]
@@ -157,21 +175,16 @@ def tile_attend_labelforward_kernel(tc, hid, voc_words, voc_scales, old, skip, o
         nc.vector.reciprocal(inv[:], total[:])
 
         w = sb.tile([P, V], F32, name="w")
-        last = CHUNKS - 1
-        last_factor = sb.tile([P, 1], F32, name="last_factor")
-        nc.scalar.activation(last_factor[:], lift[:, last : last + 1], ACT.Copy, scale=inv[:])
-        nc.scalar.activation(w[:, last * N :], exps[last][:], ACT.Copy, scale=last_factor[:])
-        for c in range(last):
-            nc.vector.tensor_scalar(
-                w[:, c * N : (c + 1) * N], exps[c][:], lift[:, c : c + 1], inv[:], ALU.mult, ALU.mult
-            )
+        factor = sb.tile([P, 2], F32, name="factor")
+        nc.scalar.activation(factor[:], lift[:, 3:5], ACT.Copy, scale=inv[:])
+        for c, (lo, hi) in enumerate(SPANS):
+            if c < 3:
+                nc.vector.tensor_scalar(w[:, lo:hi], exps[c][:], lift[:, c : c + 1], inv[:], ALU.mult, ALU.mult)
+            else:
+                nc.scalar.activation(w[:, lo:hi], exps[c][:], ACT.Copy, scale=factor[:, c - 3 : c - 2])
 
-        piece = L // OUT_PIECES
-        for h in range(OUT_PIECES):
-            res = sb.tile([P, piece], F32, name=f"res{h}")
-            cols = slice(h * piece // LIST_COL, (h + 1) * piece // LIST_COL)
-            nc.vector.tensor_tensor(
-                res[:], w[:].indirect(label_list[:, cols]), reach[:, h * piece : (h + 1) * piece], ALU.mult
-            )
-            queue = nc.sync if h == OUT_PIECES - 1 else nc.scalar
-            queue.dma_start(out[:, h * piece : (h + 1) * piece], res[:])
+        for h, (lo, hi) in enumerate(OUT_PIECES):
+            res = sb.tile([P, hi - lo], F32, name=f"res{h}")
+            nc.vector.tensor_tensor(res[:], w[:].indirect(label_list[:, listed(lo, hi)]), reach[:, lo:hi], ALU.mult)
+            queue = nc.scalar if h == 0 else nc.sync
+            queue.dma_start(out[:, lo:hi], res[:])

@@ -22,6 +22,7 @@ PACK = 4
 LIST_COL = 16
 PAD = 8
 ROW0 = P - 16
+SKIP0 = P - L // P
 SCALE_GATHERS = 2
 SPANS = ((0, 512), (512, 1024), (1024, 1536), (1536, 1792), (1792, 2048))
 OUT_PIECES = ((0, 384), (384, 512))
@@ -56,16 +57,15 @@ def tile_attend_labelforward_kernel(tc, hid, voc_words, voc_scales, old, skip, o
         nc.scalar.dma_start(hid_raw[:], hid.rearrange("(p t) q -> p t q", t=PACK))
         nc.scalar.dma_start(old_pad[:, PAD:], old)
         nc.scalar.dma_start(word_store[:].bitcast(I32), voc_words[0].bitcast(I32))
+        nc.sync.dma_start(skip_rows[SKIP0:, :], skip.rearrange("o (j p) -> (o j) p", p=P))
         nc.sync.dma_start(label_list[:], offs2)
 
-        nc.vector.memset(scale_store[0:ROW0, :].bitcast(I32), 0)
-        nc.vector.memset(old_pad[:, 0:PAD], 0.0)
-
-        nc.vector.memset(voc_plane[:].bitcast(I32), 0)
-        nc.vector.memset(skip_rows[:], 0.0)
         nc.vector.memset(ident[:], 0.0)
         make_identity(nc, ident[:], nomemset=True)
-        nc.sync.dma_start(skip_rows[0 : L // P, :], skip.rearrange("o (j p) -> (o j) p", p=P))
+        nc.vector.memset(scale_store[0:ROW0, :].bitcast(I32), 0)
+        nc.vector.memset(skip_rows[0:SKIP0, :], 0.0)
+        nc.vector.memset(old_pad[:, 0:PAD], 0.0)
+        nc.vector.memset(voc_plane[:].bitcast(I32), 0)
 
         hid_grouped = sb.tile([P, Q, PACK], BF16, name="hid_grouped", tag="words_a", align_bytes=64)
         nc.scalar.copy(hid_grouped[:], hid_raw[:].rearrange("p t q -> p q t"))
@@ -94,7 +94,7 @@ def tile_attend_labelforward_kernel(tc, hid, voc_words, voc_scales, old, skip, o
         skip_ps = ps.tile([P, P], F32, name="skip_ps", tag="reach_ps")
         nc.tensor.transpose(skip_ps[:], skip_rows[:], ident[:])
         skip_cols = sb.tile([P, L // P], F32, name="skip_cols")
-        nc.scalar.copy(skip_cols[:], skip_ps[:, 0 : L // P])
+        nc.scalar.copy(skip_cols[:], skip_ps[:, SKIP0:])
 
         far_ps = ps.tile([P, L], F32, name="far_ps")
         near_ps = ps.tile([P, L], F32, name="near_ps")

@@ -52,12 +52,12 @@ def tile_attend_labelforward_kernel(tc, hid, voc_words, voc_scales, old, skip, o
         hid_raw = sb.tile([P, PACK, Q], F32, name="hid_raw", tag="stage1", align_bytes=64)
 
         word_store = sb.tile([P, T], U16, name="word_store", align_bytes=64)
+        nc.sync.dma_start(scale_store[ROW0:, :].bitcast(I32), voc_scales[0].bitcast(I32))
         nc.sync.dma_start(entry_list[:], offs)
-        nc.scalar.dma_start(scale_store[ROW0:, :].bitcast(I32), voc_scales[0].bitcast(I32))
-        nc.scalar.dma_start(hid_raw[:], hid.rearrange("(p t) q -> p t q", t=PACK))
-        nc.scalar.dma_start(old_pad[:, PAD:], old)
-        nc.scalar.dma_start(word_store[:].bitcast(I32), voc_words[0].bitcast(I32))
+        nc.sync.dma_start(hid_raw[:], hid.rearrange("(p t) q -> p t q", t=PACK))
         nc.sync.dma_start(skip_rows[SKIP0:, :], skip.rearrange("o (j p) -> (o j) p", p=P))
+        nc.sync.dma_start(old_pad[:, PAD:], old)
+        nc.sync.dma_start(word_store[:].bitcast(I32), voc_words[0].bitcast(I32))
         nc.sync.dma_start(label_list[:], offs2)
 
         nc.vector.memset(ident[:], 0.0)
@@ -153,11 +153,11 @@ def tile_attend_labelforward_kernel(tc, hid, voc_words, voc_scales, old, skip, o
             nc.scalar.activation(e[:], score[:], ACT.Exp, bias=neg_max[:, c : c + 1], accum_out=sums[:, c : c + 1])
             exps.append(e)
 
-        first = gather_words(0, 1024, "words_a")
-        second = gather_words(1024, 1536, "stage0")
+        first = gather_words(0, 512, "words_a")
+        second = gather_words(512, 1536, "stage0")
         score_span(0, first)
-        score_span(1, first)
         third = gather_words(1536, 2048, "words_a")
+        score_span(1, second)
         score_span(2, second)
         score_span(3, third)
         score_span(4, third)

@@ -19,13 +19,17 @@ AXIS_X = mybir.AxisListType.X
 
 P = 128
 PACK = 4
+QUADRANT = 32
+ROWS_PER_QUADRANT = 4
 LIST_COL = 16
 PAD = 8
-ROW0 = P - 16
-SKIP0 = P - L // P
-SCALE_GATHERS = 2
-SPANS = ((0, 512), (512, 1024), (1024, 1536), (1536, 1792), (1792, 2048))
-OUT_PIECES = ((0, 384), (384, 512))
+LABEL_TILES = L // P
+SCALE_ROW0 = P - D // 32
+SKIP_ROW0 = P - LABEL_TILES
+SPAN = 512
+SPANS = V // SPAN
+SCALE_HALF = V // 2
+OUT_PIECES = ((0, 384), (384, L))
 
 FLOPS = 2 * D * Q * V
 
@@ -50,34 +54,34 @@ def tile_attend_labelforward_kernel(tc, hid, voc_words, voc_scales, old, skip, o
         ident = sb.tile([P, P], F32, name="ident")
         voc_plane = sb.tile([P, V], U8, name="voc_plane", align_bytes=64)
         hid_raw = sb.tile([P, PACK, Q], F32, name="hid_raw", tag="stage1", align_bytes=64)
-
         word_store = sb.tile([P, T], U16, name="word_store", align_bytes=64)
-        nc.sync.dma_start(scale_store[ROW0:, :].bitcast(I32), voc_scales[0].bitcast(I32))
+
+        nc.sync.dma_start(scale_store[SCALE_ROW0:, :].bitcast(I32), voc_scales[0].bitcast(I32))
         nc.sync.dma_start(entry_list[:], offs)
         nc.sync.dma_start(hid_raw[:], hid.rearrange("(p t) q -> p t q", t=PACK))
-        nc.sync.dma_start(skip_rows[SKIP0:, :], skip.rearrange("o (j p) -> (o j) p", p=P))
+        nc.sync.dma_start(skip_rows[SKIP_ROW0:, :], skip.rearrange("o (j p) -> (o j) p", p=P))
         nc.sync.dma_start(old_pad[:, PAD:], old)
         nc.sync.dma_start(word_store[:].bitcast(I32), voc_words[0].bitcast(I32))
         nc.sync.dma_start(label_list[:], offs2)
 
         nc.vector.memset(ident[:], 0.0)
         make_identity(nc, ident[:], nomemset=True)
-        nc.vector.memset(scale_store[0:ROW0, :].bitcast(I32), 0)
-        nc.vector.memset(skip_rows[0:SKIP0, :], 0.0)
+        nc.vector.memset(scale_store[0:SCALE_ROW0, :].bitcast(I32), 0)
+        nc.vector.memset(skip_rows[0:SKIP_ROW0, :], 0.0)
         nc.vector.memset(old_pad[:, 0:PAD], 0.0)
         nc.vector.memset(voc_plane[:].bitcast(I32), 0)
 
         hid_grouped = sb.tile([P, Q, PACK], BF16, name="hid_grouped", tag="words_a", align_bytes=64)
         nc.scalar.copy(hid_grouped[:], hid_raw[:].rearrange("p t q -> p q t"))
 
-        def gather_scales(g):
-            width = V // SCALE_GATHERS
-            lo, hi = g * width, (g + 1) * width
-            picked_scales = sb.tile([P, width], U8, name=f"picked_scales{g}", tag=f"stage{g}", align_bytes=64)
-            nc.vector.tensor_copy(picked_scales[:], scale_store[:].indirect(entry_list[:, listed(lo, hi)]))
-            for j in range(4):
+        def gather_scales(half):
+            lo, hi = half * SCALE_HALF, (half + 1) * SCALE_HALF
+            picked = sb.tile([P, SCALE_HALF], U8, name=f"picked{half}", tag=f"stage{half}", align_bytes=64)
+            nc.vector.tensor_copy(picked[:], scale_store[:].indirect(entry_list[:, listed(lo, hi)]))
+            for j in range(ROWS_PER_QUADRANT):
                 nc.sync.dma_start(
-                    voc_plane[j:P:32, lo:hi].bitcast(I32), picked_scales[ROW0 + j : P : 4, :].bitcast(I32)
+                    voc_plane[j:P:QUADRANT, lo:hi].bitcast(I32),
+                    picked[SCALE_ROW0 + j : P : ROWS_PER_QUADRANT, :].bitcast(I32),
                 )
 
         gather_scales(0)
@@ -90,18 +94,17 @@ def tile_attend_labelforward_kernel(tc, hid, voc_words, voc_scales, old, skip, o
         )
         gather_scales(1)
 
-
         skip_ps = ps.tile([P, P], F32, name="skip_ps", tag="reach_ps")
         nc.tensor.transpose(skip_ps[:], skip_rows[:], ident[:])
-        skip_cols = sb.tile([P, L // P], F32, name="skip_cols")
-        nc.scalar.copy(skip_cols[:], skip_ps[:, SKIP0:])
+        skip_cols = sb.tile([P, LABEL_TILES], F32, name="skip_cols")
+        nc.scalar.copy(skip_cols[:], skip_ps[:, SKIP_ROW0:])
 
         far_ps = ps.tile([P, L], F32, name="far_ps")
         near_ps = ps.tile([P, L], F32, name="near_ps")
-        for j in range(L // P):
+        for j in range(LABEL_TILES):
             lo = PAD + j * P
             nc.tensor.transpose(far_ps[:, j * P : (j + 1) * P], old_pad[:, lo - 2 : lo - 2 + P], ident[:])
-        for j in range(L // P):
+        for j in range(LABEL_TILES):
             lo = PAD + j * P
             for back in range(2):
                 nc.tensor.matmul(
@@ -114,59 +117,59 @@ def tile_attend_labelforward_kernel(tc, hid, voc_words, voc_scales, old, skip, o
                 )
         far_t = sb.tile([P, L], F32, name="far_t")
         near_t = sb.tile([P, L], F32, name="near_t")
-        for j in range(L // P):
+        for j in range(LABEL_TILES):
             blk = slice(j * P, (j + 1) * P)
             nc.scalar.activation(far_t[:, blk], far_ps[:, blk], ACT.Copy, scale=skip_cols[:, j : j + 1])
         nc.scalar.copy(near_t[:], near_ps[:])
         reach_ps = ps.tile([P, L], F32, name="reach_ps", tag="reach_ps")
-        for j in range(L // P):
+        for j in range(LABEL_TILES):
             blk = slice(j * P, (j + 1) * P)
             nc.tensor.matmul(reach_ps[:, blk], near_t[:, blk], ident[:], start=True, stop=False, is_transpose=True)
             nc.tensor.matmul(reach_ps[:, blk], far_t[:, blk], ident[:], start=False, stop=True, is_transpose=True)
         reach = sb.tile([P, L], F32, name="reach")
         nc.scalar.copy(reach[:], reach_ps[:])
 
-        neg_max = sb.tile([P, len(SPANS)], F32, name="neg_max")
-        sums = sb.tile([P, len(SPANS)], F32, name="sums")
+        neg_max = sb.tile([P, SPANS], F32, name="neg_max")
+        sums = sb.tile([P, SPANS], F32, name="sums")
         exps = []
 
-        def gather_words(lo, hi, tag):
-            words = sb.tile([P, hi - lo], U16, name=f"words{lo}", tag=tag, align_bytes=64)
+        def gather_words(first_span, spans, tag):
+            lo, hi = first_span * SPAN, (first_span + spans) * SPAN
+            words = sb.tile([P, hi - lo], U16, name=f"words{first_span}", tag=tag, align_bytes=64)
             nc.vector.tensor_copy(words[:], word_store[:].indirect(entry_list[:, listed(lo, hi)]))
-            return words, lo
+            return [words[:, s * SPAN : (s + 1) * SPAN] for s in range(spans)]
 
-        def score_span(c, gathered):
-            words, base = gathered
-            lo, hi = SPANS[c]
-            score = ps.tile([P, hi - lo], F32, name=f"score{c}")
+        def score_span(c, span_words):
+            score = ps.tile([P, SPAN], F32, name=f"score{c}")
             nc.tensor.matmul_mx(
                 out=score[:],
                 lhsT=hid_codes[:].bitcast(FP8X4),
                 lhsT_scale=hid_plane[:],
-                rhs=words[:, lo - base : hi - base].bitcast(FP4X4),
-                rhs_scale=voc_plane[:, lo:hi],
+                rhs=span_words.bitcast(FP4X4),
+                rhs_scale=voc_plane[:, c * SPAN : (c + 1) * SPAN],
                 start=True,
                 stop=True,
             )
             nc.vector.tensor_reduce(neg_max[:, c : c + 1], score[:], AXIS_X, ALU.max, negate=True)
-            e = sb.tile([P, hi - lo], F32, name=f"exp{c}")
-            nc.scalar.activation(e[:], score[:], ACT.Exp, bias=neg_max[:, c : c + 1], accum_out=sums[:, c : c + 1])
-            exps.append(e)
+            span_exp = sb.tile([P, SPAN], F32, name=f"exp{c}")
+            nc.scalar.activation(
+                span_exp[:], score[:], ACT.Exp, bias=neg_max[:, c : c + 1], accum_out=sums[:, c : c + 1]
+            )
+            exps.append(span_exp)
 
-        first = gather_words(0, 512, "words_a")
-        second = gather_words(512, 1536, "stage0")
-        score_span(0, first)
-        third = gather_words(1536, 2048, "words_a")
-        score_span(1, second)
-        score_span(2, second)
-        score_span(3, third)
-        score_span(4, third)
+        words_0 = gather_words(0, 1, "words_a")
+        words_12 = gather_words(1, 2, "stage0")
+        score_span(0, words_0[0])
+        words_3 = gather_words(3, 1, "words_a")
+        score_span(1, words_12[0])
+        score_span(2, words_12[1])
+        score_span(3, words_3[0])
 
         neg_top = sb.tile([P, 1], F32, name="neg_top")
         nc.vector.tensor_reduce(neg_top[:], neg_max[:], AXIS_X, ALU.min)
-        lift = sb.tile([P, len(SPANS)], F32, name="lift")
+        lift = sb.tile([P, SPANS], F32, name="lift")
         nc.scalar.activation(lift[:], neg_max[:], ACT.Exp, bias=neg_top[:], scale=-1.0)
-        shares = sb.tile([P, len(SPANS)], F32, name="shares")
+        shares = sb.tile([P, SPANS], F32, name="shares")
         total = sb.tile([P, 1], F32, name="total")
         nc.vector.scalar_tensor_tensor(
             shares[:], sums[:], 1.0 / V, lift[:], ALU.mult, ALU.mult, accum_out=total[:]
@@ -175,16 +178,16 @@ def tile_attend_labelforward_kernel(tc, hid, voc_words, voc_scales, old, skip, o
         nc.vector.reciprocal(inv[:], total[:])
 
         w = sb.tile([P, V], F32, name="w")
-        factor = sb.tile([P, 2], F32, name="factor")
-        nc.scalar.activation(factor[:], lift[:, 3:5], ACT.Copy, scale=inv[:])
-        for c, (lo, hi) in enumerate(SPANS):
-            if c < 3:
-                nc.vector.tensor_scalar(w[:, lo:hi], exps[c][:], lift[:, c : c + 1], inv[:], ALU.mult, ALU.mult)
-            else:
-                nc.scalar.activation(w[:, lo:hi], exps[c][:], ACT.Copy, scale=factor[:, c - 3 : c - 2])
+        last = SPANS - 1
+        last_factor = sb.tile([P, 1], F32, name="last_factor")
+        nc.scalar.activation(last_factor[:], lift[:, last:], ACT.Copy, scale=inv[:])
+        for c in range(last):
+            nc.vector.tensor_scalar(
+                w[:, c * SPAN : (c + 1) * SPAN], exps[c][:], lift[:, c : c + 1], inv[:], ALU.mult, ALU.mult
+            )
+        nc.scalar.activation(w[:, last * SPAN :], exps[last][:], ACT.Copy, scale=last_factor[:])
 
-        for h, (lo, hi) in enumerate(OUT_PIECES):
-            res = sb.tile([P, hi - lo], F32, name=f"res{h}")
+        for (lo, hi), queue in zip(OUT_PIECES, (nc.scalar, nc.sync)):
+            res = sb.tile([P, hi - lo], F32, name=f"res{lo}")
             nc.vector.tensor_tensor(res[:], w[:].indirect(label_list[:, listed(lo, hi)]), reach[:, lo:hi], ALU.mult)
-            queue = nc.scalar if h == 0 else nc.sync
             queue.dma_start(out[:, lo:hi], res[:])

from contextlib import ExitStack

import concourse.mybir as mybir
from concourse.masks import make_identity

D, V, L, Q, T = 512, 2048, 512, 128, 4096

F32 = mybir.dt.float32
BF16 = mybir.dt.bfloat16
I32 = mybir.dt.int32
U32 = mybir.dt.uint32
U16 = mybir.dt.uint16
U8 = mybir.dt.uint8
FP8X4 = mybir.dt.float8_e4m3fn_x4
FP4X4 = mybir.dt.float4_e2m1fn_x4
ALU = mybir.AluOpType
ACT = mybir.ActivationFunctionType
AXIS_X = mybir.AxisListType.X

P = 128
PACK = 4
QUADRANT = 32
ROWS_PER_QUADRANT = 4
LIST_COL = 16
PAD = 8
LABEL_TILES = L // P
SCALE_ROW0 = P - D // 32
SKIP_ROW0 = P - LABEL_TILES
SPAN = 512
SPANS = V // SPAN
SCALE_HALF = V // 2
OUT_PIECES = ((0, 384), (384, L))

FLOPS = 2 * D * Q * V


def listed(lo, hi):
    return slice(lo // LIST_COL, hi // LIST_COL)


def tile_attend_labelforward_kernel(tc, hid, voc_words, voc_scales, old, skip, offs, offs2, out):
    nc = tc.nc
    with ExitStack() as ctx:
        lists = ctx.enter_context(tc.tile_pool(name="lists", bufs=1))
        sb = ctx.enter_context(tc.tile_pool(name="sb", bufs=1))
        ps = ctx.enter_context(tc.psum_pool(name="ps", bufs=1))

        entry_list = lists.tile([P, V // LIST_COL], U16, name="entry_list")
        label_list = lists.tile([P, L // LIST_COL], U16, name="label_list")

        scale_store = sb.tile([P, T], U8, name="scale_store", align_bytes=64)
        old_pad = sb.tile([P, PAD + L], F32, name="old_pad")
        skip_rows = sb.tile([P, P], F32, name="skip_rows")
        ident = sb.tile([P, P], F32, name="ident")
        voc_plane = sb.tile([P, V], U8, name="voc_plane", align_bytes=64)
        hid_raw = sb.tile([P, PACK, Q], F32, name="hid_raw", tag="stage1", align_bytes=64)
        word_store = sb.tile([P, T], U16, name="word_store", align_bytes=64)

        nc.sync.dma_start(scale_store[SCALE_ROW0:, :].bitcast(I32), voc_scales[0].bitcast(I32))
        nc.sync.dma_start(entry_list[:], offs)
        nc.sync.dma_start(hid_raw[:], hid.rearrange("(p t) q -> p t q", t=PACK))
        nc.sync.dma_start(skip_rows[SKIP_ROW0:, :], skip.rearrange("o (j p) -> (o j) p", p=P))
        nc.sync.dma_start(old_pad[:, PAD:], old)
        nc.sync.dma_start(word_store[:].bitcast(I32), voc_words[0].bitcast(I32))
        nc.sync.dma_start(label_list[:], offs2)

        nc.vector.memset(ident[:], 0.0)
        make_identity(nc, ident[:], nomemset=True)
        nc.vector.memset(scale_store[0:SCALE_ROW0, :].bitcast(I32), 0)
        nc.vector.memset(skip_rows[0:SKIP_ROW0, :], 0.0)
        nc.vector.memset(old_pad[:, 0:PAD], 0.0)
        nc.vector.memset(voc_plane[:].bitcast(I32), 0)

        hid_grouped = sb.tile([P, Q, PACK], BF16, name="hid_grouped", tag="words_a", align_bytes=64)
        nc.scalar.copy(hid_grouped[:], hid_raw[:].rearrange("p t q -> p q t"))

        def gather_scales(half):
            lo, hi = half * SCALE_HALF, (half + 1) * SCALE_HALF
            picked = sb.tile([P, SCALE_HALF], U8, name=f"picked{half}", tag=f"stage{half}", align_bytes=64)
            nc.vector.tensor_copy(picked[:], scale_store[:].indirect(entry_list[:, listed(lo, hi)]))
            for j in range(ROWS_PER_QUADRANT):
                nc.sync.dma_start(
                    voc_plane[j:P:QUADRANT, lo:hi].bitcast(I32),
                    picked[SCALE_ROW0 + j : P : ROWS_PER_QUADRANT, :].bitcast(I32),
                )

        gather_scales(0)
        hid_codes = sb.tile([P, Q], U32, name="hid_codes", align_bytes=64)
        hid_plane = sb.tile([P, Q], U8, name="hid_plane", align_bytes=64)
        nc.vector.quantize_mx(
            out=hid_codes[:].bitcast(FP8X4),
            scales=hid_plane[:],
            in_=hid_grouped[:].rearrange("p q t -> p (q t)"),
        )
        gather_scales(1)

        skip_ps = ps.tile([P, P], F32, name="skip_ps", tag="reach_ps")
        nc.tensor.transpose(skip_ps[:], skip_rows[:], ident[:])
        skip_cols = sb.tile([P, LABEL_TILES], F32, name="skip_cols")
        nc.scalar.copy(skip_cols[:], skip_ps[:, SKIP_ROW0:])

        far_ps = ps.tile([P, L], F32, name="far_ps")
        near_ps = ps.tile([P, L], F32, name="near_ps")
        for j in range(LABEL_TILES):
            lo = PAD + j * P
            nc.tensor.transpose(far_ps[:, j * P : (j + 1) * P], old_pad[:, lo - 2 : lo - 2 + P], ident[:])
        for j in range(LABEL_TILES):
            lo = PAD + j * P
            for back in range(2):
                nc.tensor.matmul(
                    near_ps[:, j * P : (j + 1) * P],
                    old_pad[:, lo - back : lo - back + P],
                    ident[:],
                    start=(back == 0),
                    stop=(back == 1),
                    is_transpose=True,
                )
        far_t = sb.tile([P, L], F32, name="far_t")
        near_t = sb.tile([P, L], F32, name="near_t")
        for j in range(LABEL_TILES):
            blk = slice(j * P, (j + 1) * P)
            nc.scalar.activation(far_t[:, blk], far_ps[:, blk], ACT.Copy, scale=skip_cols[:, j : j + 1])
        nc.scalar.copy(near_t[:], near_ps[:])
        reach_ps = ps.tile([P, L], F32, name="reach_ps", tag="reach_ps")
        for j in range(LABEL_TILES):
            blk = slice(j * P, (j + 1) * P)
            nc.tensor.matmul(reach_ps[:, blk], near_t[:, blk], ident[:], start=True, stop=False, is_transpose=True)
            nc.tensor.matmul(reach_ps[:, blk], far_t[:, blk], ident[:], start=False, stop=True, is_transpose=True)
        reach = sb.tile([P, L], F32, name="reach")
        nc.scalar.copy(reach[:], reach_ps[:])

        neg_max = sb.tile([P, SPANS], F32, name="neg_max")
        sums = sb.tile([P, SPANS], F32, name="sums")
        exps = []

        def gather_words(first_span, spans, tag):
            lo, hi = first_span * SPAN, (first_span + spans) * SPAN
            words = sb.tile([P, hi - lo], U16, name=f"words{first_span}", tag=tag, align_bytes=64)
            nc.vector.tensor_copy(words[:], word_store[:].indirect(entry_list[:, listed(lo, hi)]))
            return [words[:, s * SPAN : (s + 1) * SPAN] for s in range(spans)]

        def score_span(c, span_words):
            score = ps.tile([P, SPAN], F32, name=f"score{c}")
            nc.tensor.matmul_mx(
                out=score[:],
                lhsT=hid_codes[:].bitcast(FP8X4),
                lhsT_scale=hid_plane[:],
                rhs=span_words.bitcast(FP4X4),
                rhs_scale=voc_plane[:, c * SPAN : (c + 1) * SPAN],
                start=True,
                stop=True,
            )
            nc.vector.tensor_reduce(neg_max[:, c : c + 1], score[:], AXIS_X, ALU.max, negate=True)
            span_exp = sb.tile([P, SPAN], F32, name=f"exp{c}")
            nc.scalar.activation(
                span_exp[:], score[:], ACT.Exp, bias=neg_max[:, c : c + 1], accum_out=sums[:, c : c + 1]
            )
            exps.append(span_exp)

        words_0 = gather_words(0, 1, "words_a")
        words_12 = gather_words(1, 2, "stage0")
        score_span(0, words_0[0])
        words_3 = gather_words(3, 1, "words_a")
        score_span(1, words_12[0])
        score_span(2, words_12[1])
        score_span(3, words_3[0])

        neg_top = sb.tile([P, 1], F32, name="neg_top")
        nc.vector.tensor_reduce(neg_top[:], neg_max[:], AXIS_X, ALU.min)
        lift = sb.tile([P, SPANS], F32, name="lift")
        nc.scalar.activation(lift[:], neg_max[:], ACT.Exp, bias=neg_top[:], scale=-1.0)
        shares = sb.tile([P, SPANS], F32, name="shares")
        total = sb.tile([P, 1], F32, name="total")
        nc.vector.scalar_tensor_tensor(
            shares[:], sums[:], 1.0 / V, lift[:], ALU.mult, ALU.mult, accum_out=total[:]
        )
        inv = sb.tile([P, 1], F32, name="inv")
        nc.vector.reciprocal(inv[:], total[:])

        w = sb.tile([P, V], F32, name="w")
        last = SPANS - 1
        last_factor = sb.tile([P, 1], F32, name="last_factor")
        nc.scalar.activation(last_factor[:], lift[:, last:], ACT.Copy, scale=inv[:])
        for c in range(last):
            nc.vector.tensor_scalar(
                w[:, c * SPAN : (c + 1) * SPAN], exps[c][:], lift[:, c : c + 1], inv[:], ALU.mult, ALU.mult
            )
        nc.scalar.activation(w[:, last * SPAN :], exps[last][:], ACT.Copy, scale=last_factor[:])

        for (lo, hi), queue in zip(OUT_PIECES, (nc.scalar, nc.sync)):
            res = sb.tile([P, hi - lo], F32, name=f"res{lo}")
            nc.vector.tensor_tensor(res[:], w[:].indirect(label_list[:, listed(lo, hi)]), reach[:, lo:hi], ALU.mult)
            queue.dma_start(out[:, lo:hi], res[:])
